import numpy as np
import ml_dtypes


def mxq(x, axis, fmt="e4m3"):
    dtype, down = {"e4m3": (ml_dtypes.float8_e4m3fn, 7), "e5m2": (ml_dtypes.float8_e5m2, 14)}[fmt]
    v = np.moveaxis(np.asarray(x, np.float32).astype(ml_dtypes.bfloat16).astype(np.float64), axis, -1)
    blocks = v.reshape(v.shape[:-1] + (-1, 32))
    amax = np.abs(blocks).max(-1, keepdims=True)
    byte = np.maximum(np.where(amax > 0, np.frexp(amax)[1] - 1 + 127, 0) - down, 1)
    scale = np.exp2(byte - 127.0)
    codes = (blocks / scale).astype(np.float32).astype(dtype).astype(np.float64)
    return np.moveaxis((codes * scale).reshape(v.shape), -1, axis)


WIDE = False


def mx_kscale(k):
    if not WIDE:
        return np.ones(k)
    levels = np.array([30, -30])
    if k % 512:
        return np.exp2(np.random.permutation(np.resize(levels, k // 32))).repeat(32)
    a = np.empty((k // 512, 16))
    for p in range(k // 512):
        a[p, :8] = np.random.permutation(np.resize(levels, 8))
        for g in range(8):
            far = levels[np.abs(levels - a[p, g]) >= 10]
            a[p, g + 8] = far[np.random.randint(len(far))]
    return np.exp2(a.ravel()).repeat(32)


def f64(x):
    return np.asarray(x).astype(np.float64)


def striped(idx):
    return np.tile(np.asarray(idx).reshape(-1, 16).T, (8, 1)).astype(np.uint16)


def unstriped(offs):
    return offs[:16].T.reshape(-1).astype(np.int64)


def striped8(idx):
    return np.asarray(idx).reshape(8, -1, 16).transpose(0, 2, 1).reshape(128, -1).astype(np.uint16)


def unstriped8(offs):
    return offs.reshape(8, 16, -1).transpose(0, 2, 1).reshape(8, -1).astype(np.int64)


def pick8(x, idx, run):
    r = np.arange(len(x))
    return x[r[:, None], idx[r % (8 * run) // run]]


E2M1 = np.array([0.0, 0.5, 1.0, 1.5, 2.0, 3.0, 4.0, 6.0, -0.0, -0.5, -1.0, -1.5, -2.0, -3.0, -4.0, -6.0])


def pack_weight(w, fmt):
    k, n = w.shape
    w = f64(np.asarray(w, np.float32).astype(ml_dtypes.bfloat16)).reshape(k // 32, 32, n)
    amax = np.abs(w).max(1)
    if fmt in ("e4m3", "e5m2"):
        byte = np.frexp(amax)[1] - 1 + 127 - (7 if fmt == "e4m3" else 14)
    else:
        mant, ex = np.frexp(amax / 6.0)
        byte = np.where(mant > 0.5, ex, ex - 1) + 127
    byte = np.clip(np.where(amax > 0, byte, 1), 1, 254)
    scaled = (w * np.exp2(127.0 - byte)[:, None, :]).reshape(k, n).astype(np.float32)
    by_word = np.ascontiguousarray(scaled.reshape(k // 512, 128, 4, n).transpose(0, 1, 3, 2))
    if fmt in ("e4m3", "e5m2"):
        words = by_word.astype(ml_dtypes.float8_e4m3fn if fmt == "e4m3" else ml_dtypes.float8_e5m2).view(np.uint8)
    else:
        c = by_word.astype(ml_dtypes.float4_e2m1fn).view(np.uint8) & 0xF
        words = (c[..., 0::2] | (c[..., 1::2] << 4)).reshape(k // 512, 128, 2 * n)
    return np.ascontiguousarray(words), np.ascontiguousarray(byte.astype(np.uint8).reshape(k // 512, 16, n))


def unpack_weight(words, scales, fmt):
    g, _, n = scales.shape
    words = np.ascontiguousarray(words).reshape(g, 128, n, -1)
    if fmt in ("e4m3", "e5m2"):
        vals = words.view(ml_dtypes.float8_e4m3fn if fmt == "e4m3" else ml_dtypes.float8_e5m2).astype(np.float64)
    else:
        nib = np.empty((g, 128, n, 4), np.uint8)
        nib[..., 0::2] = words & 0xF
        nib[..., 1::2] = words >> 4
        vals = E2M1[nib]
    vals = vals * np.repeat(np.exp2(scales.astype(np.float64) - 127.0), 8, axis=1)[..., None]
    return vals.transpose(0, 1, 3, 2).reshape(g * 512, n)


def sigmoid(v):
    return 1.0 / (1.0 + np.exp(-v))


def sgn(shape):
    return np.random.uniform(0.5, 2.0, shape) * np.where(np.random.standard_normal(shape) < 0, -1.0, 1.0)


K, T, J, R, C, O, N = 512, 2048, 256, 512, 512, 128, 256


def setup_inputs():
    n = np.random.standard_normal
    idx = np.random.permutation(T)[:J]
    idx2 = np.random.permutation(T)[:J]
    idx3 = np.stack([np.random.permutation(C)[:J] for _ in range(8)])
    idx4 = np.random.permutation(C)[:O]
    idx5 = np.stack([np.random.permutation(J)[:O] for _ in range(8)])
    fk = mx_kscale(K)
    fr = mx_kscale(R)
    xtp = pack_weight(n((K, T)) / fk[:, None], "e2m1")
    wp = pack_weight(n((K, R)) * 1 / np.sqrt(K) * fk[:, None] * fr, "e5m2")
    w2p = pack_weight(n((K, R)) * 1 / np.sqrt(K) * fk[:, None], "e4m3")
    wbp = pack_weight(n((R, N)) * 1 / np.sqrt(R) / fr[:, None], "e4m3")
    return {
        "xt_words": xtp[0],
        "xt_scales": xtp[1],
        "w_words": wp[0],
        "w_scales": wp[1],
        "w2_words": w2p[0],
        "w2_scales": w2p[1],
        "sa": (sgn((R, 1))).astype(np.float32),
        "sg": (sgn((R, 1))).astype(np.float32),
        "bg": (np.random.uniform(-2.0, 2.0, (R, 1))).astype(np.float32),
        "wb_words": wbp[0],
        "wb_scales": wbp[1],
        "offs": striped(idx),
        "offs2": striped(idx2),
        "offs3": striped8(idx3),
        "offs4": striped(idx4),
        "offs5": striped8(idx5),
    }


def reference(xt_words, xt_scales, w_words, w_scales, w2_words, w2_scales, sa, sg, bg, wb_words, wb_scales, offs, offs2, offs3, offs4, offs5):
    idx = unstriped(offs)
    idx2 = unstriped(offs2)
    idx3 = unstriped8(offs3)
    idx4 = unstriped(offs4)
    idx5 = unstriped8(offs5)
    xtu = unpack_weight(xt_words, xt_scales, "e2m1")
    wu = unpack_weight(w_words, w_scales, "e5m2")
    w2u = unpack_weight(w2_words, w2_scales, "e4m3")
    wbu = unpack_weight(wb_words, wb_scales, "e4m3")
    xtidxg = xtu[:, idx]
    a = wu.T @ xtidxg
    xtidx2g = xtu[:, idx2]
    b = w2u.T @ xtidx2g
    pa = np.zeros((R, C))
    pa[np.arange(R)[:, None], idx3[np.arange(R) % 512 // 64]] = a
    hid = pa[:, idx4] * f64(sa) * sigmoid(pick8(b, idx5, 64) * f64(sg) + f64(bg))
    hidq = mxq(hid, 0, "e4m3")
    p = wbu.T @ hidq
    return p

@@ -1,0 +1,208 @@
+from contextlib import ExitStack
+
+import concourse.mybir as mybir
+
+K, T, J, R, C, O, N = 512, 2048, 256, 512, 512, 128, 256
+FLOPS = 2 * K * R * J * 2 + 2 * R * N * O
+
+F32 = mybir.dt.float32
+BF16 = mybir.dt.bfloat16
+I32 = mybir.dt.int32
+U32 = mybir.dt.uint32
+U16 = mybir.dt.uint16
+U8 = mybir.dt.uint8
+E4M3 = mybir.dt.float8_e4m3fn_x4
+E5M2 = mybir.dt.float8_e5m2_x4
+E2M1 = mybir.dt.float4_e2m1fn_x4
+ACT = mybir.ActivationFunctionType
+MULT = mybir.AluOpType.mult
+
+P = 128
+PACK = 4
+QUADS = 4
+QUAD = 32
+
+
+def tile_list_gatedbyslots_kernel(tc, xt_words, xt_scales, w_words, w_scales, w2_words, w2_scales, sa, sg, bg,
+                                      wb_words, wb_scales, offs, offs2, offs3, offs4, offs5, out):
+    nc = tc.nc
+    with ExitStack() as ctx:
+        sb = ctx.enter_context(tc.tile_pool(name="sb", bufs=1))
+        shared = ctx.enter_context(tc.tile_pool(name="shared", bufs=1))
+        ps = ctx.enter_context(tc.psum_pool(name="ps", bufs=1))
+
+        def tile(name, shape, dtype, tag=""):
+            return sb.tile(shape, dtype, name=name, tag=tag, align_bytes=64)
+
+        def load_list(name, src):
+            lst = tile(name, list(src.shape), U16)
+            nc.sync.dma_start(lst[:], src)
+            return lst
+
+        def load_words(name, src, queue, tag=""):
+            cols = src.shape[2]
+            words = tile(name, [P, cols], U32, tag)
+            queue.dma_start(words[:].bitcast(I32), src[0].rearrange("p n t -> p (n t)").bitcast(I32))
+            return words
+
+        def cleared_plane(name, cols):
+            plane = tile(name, [P, cols], U8)
+            nc.vector.memset(plane[:].bitcast(I32), 0)
+            return plane
+
+        def load_plane(plane, src, queue):
+            for q in range(QUADS):
+                queue.dma_start(plane[QUAD * q : QUAD * q + 4, :].bitcast(I32), src[0, 4 * q : 4 * q + 4, :].bitcast(I32))
+
+        def load_per_row(name, src):
+            col = tile(name, [P, PACK], F32)
+            nc.gpsimd.dma_start(col[:], src.rearrange("(p t) one -> p (t one)", t=PACK))
+            return col
+
+        xt_s = cleared_plane("xt_s", T)
+        w_plane = cleared_plane("w_plane", R)
+
+        list1 = load_list("list1", offs)
+        xt_w = tile("xt_w", [P, T], U16)
+        nc.sync.dma_start(xt_w[:].bitcast(I32), xt_words[0].bitcast(I32))
+        w_staged = shared.tile([P, QUADS, R // 4], I32, name="w_staged", offset=0, align_bytes=64)
+        nc.scalar.dma_start(
+            w_staged[0:4, :, :],
+            w_scales[0].bitcast(I32).rearrange("(q r) c -> r q c", r=4),
+        )
+        load_plane(xt_s, xt_scales, nc.scalar)
+        w_raw = load_words("w_raw", w_words, nc.sync)
+        list3 = load_list("list3", offs3)
+
+        def cleared_board(t, tag=""):
+            page = tile("board%d" % t, [P, C], F32, tag)
+            nc.vector.memset(page[:], 0.0)
+            return page
+
+        board = [cleared_board(0)]
+        w2_plane = cleared_plane("w2_plane", R)
+        wb_s = cleared_plane("wb_s", N)
+        board.append(cleared_board(1))
+
+        list4 = load_list("list4", offs4)
+        sa_t = load_per_row("sa_t", sa)
+        load_plane(w2_plane, w2_scales, nc.sync)
+        w2_raw = load_words("w2_raw", w2_words, nc.sync, "w2_raw")
+        list2 = load_list("list2", offs2)
+        list5 = load_list("list5", offs5)
+        sg_t = load_per_row("sg_t", sg)
+        bg_t = load_per_row("bg_t", bg)
+        wb_w = load_words("wb_w", wb_words, nc.sync)
+        load_plane(wb_s, wb_scales, nc.sync)
+
+        w_first = tile("w_first", [P, P], U32, "first_words")
+        nc.scalar.copy(w_first[:], w_raw[:, 0:R:PACK])
+        w_rest = tile("w_rest", [P, PACK - 1, P], U32, "rest_words")
+        nc.scalar.copy(w_rest[:].rearrange("p t m -> p m t"), w_raw[:].rearrange("p (m t) -> p m t", t=PACK)[:, :, 1:PACK])
+        w_dealt = [w_first[:]] + [w_rest[:, t, :] for t in range(PACK - 1)]
+        for q in range(QUADS):
+            nc.vector.tensor_copy(w_plane[QUAD * q : QUAD * q + 4, :].bitcast(I32), w_staged[0:4, q, :])
+        w_by_slot = w_plane[:].rearrange("p (m t) -> p t m", t=PACK)
+        w_s_early = tile("w_s_early", [P, 2, P], U8, "early_scales")
+        nc.vector.tensor_copy(w_s_early[:], w_by_slot[:, 0:2, :])
+
+        xa_w = shared.tile([P, J], U16, name="xa_w", offset=0, align_bytes=64)
+        nc.vector.tensor_copy(xa_w[:], xt_w[:].indirect(list1[:]))
+        xa_s = shared.tile([P, J], U8, name="xa_s", offset=2 * J, align_bytes=64)
+        nc.vector.tensor_copy(xa_s[:], xt_s[:].indirect(list1[:]))
+
+        def first_product(t, scales):
+            acc = ps.tile([P, J], F32, name="a_ps%d" % t)
+            nc.tensor.matmul_mx(out=acc[:], lhsT=w_dealt[t].bitcast(E5M2), lhsT_scale=scales,
+                                rhs=xa_w[:].bitcast(E2M1), rhs_scale=xa_s[:], start=True, stop=True)
+            return acc
+
+        def to_sbuf(name, acc, tag=""):
+            rows = tile(name, [P, J], F32, tag)
+            nc.vector.tensor_copy(rows[:], acc)
+            return rows
+
+        a_ps = [first_product(t, w_s_early[:, t, :]) for t in range(2)]
+        a_sb = [to_sbuf("a_sb%d" % t, a_ps[t][:]) for t in range(2)]
+        w_s_late = tile("w_s_late", [P, 2, P], U8, "first_words")
+        nc.vector.tensor_copy(w_s_late[:], w_by_slot[:, 2:4, :])
+        a_ps.extend([first_product(t, w_s_late[:, t - 2, :]) for t in range(2, PACK)])
+        a_sb.append(to_sbuf("a_sb2", a_ps[2][:]))
+        board.append(cleared_board(2, "rest_words"))
+
+        xb_s = tile("xb_s", [P, J], U8, "early_scales")
+        nc.vector.tensor_copy(xb_s[:], xt_s[:].indirect(list2[:]))
+        xb_w = tile("xb_w", [P, J], U16, "first_words")
+        nc.vector.tensor_copy(xb_w[:], xt_w[:].indirect(list2[:]))
+        w2_s = tile("w2_s", [P, PACK, P], U8)
+        nc.vector.tensor_copy(w2_s[:], w2_plane[:].rearrange("p (m t) -> p t m", t=PACK))
+        w2_dealt = tile("w2_dealt", [P, PACK, P], U32)
+        nc.vector.tensor_copy(w2_dealt[:].bitcast(I32).rearrange("p t m -> p m t"),
+                              w2_raw[:].bitcast(I32).rearrange("p (m t) -> p m t", t=PACK))
+        board.append(cleared_board(3, "w2_raw"))
+        b_ps = []
+        for pair in range(PACK // 2):
+            acc = ps.tile([P, 2, J], F32, name="b_ps%d" % pair)
+            for u in range(2):
+                t = 2 * pair + u
+                nc.tensor.matmul_mx(out=acc[:, u, :], lhsT=w2_dealt[:, t, :].bitcast(E4M3), lhsT_scale=w2_s[:, t, :],
+                                    rhs=xb_w[:].bitcast(E2M1), rhs_scale=xb_s[:], start=True, stop=True)
+                b_ps.append(acc[:, u, :])
+        b_sb = [to_sbuf("b_sb%d" % t, b_ps[t], "rows%d" % t) for t in range(PACK - 1)]
+
+        picked = [tile("picked%d" % t, [P, O], F32) for t in range(PACK)]
+        gate = [tile("gate%d" % t, [P, O], F32) for t in range(PACK)]
+        hid = tile("hid", [P, O, PACK], BF16)
+
+        def put(t):
+            nc.scalar.activation(out=board[t][:].indirect(list3[:]), in_=a_sb[t][:], func=ACT.Copy)
+
+        def fetch(t, lo=0, hi=O):
+            nc.scalar.activation(out=picked[t][:, lo:hi], in_=board[t][:].indirect(list4[:, lo // 16 : hi // 16]), func=ACT.Copy,
+                                 scale=sa_t[:, t : t + 1])
+
+        def look(t):
+            nc.scalar.activation(out=gate[t][:], in_=b_sb[t][:].indirect(list5[:]), func=ACT.Sigmoid,
+                                 bias=bg_t[:, t : t + 1], scale=sg_t[:, t : t + 1])
+
+        def join(t, lo=0, hi=O):
+            nc.vector.tensor_tensor(hid[:, lo:hi, t], picked[t][:, lo:hi], gate[t][:, lo:hi], MULT)
+
+        last = PACK - 1
+        put(0)
+        for t in range(1, last):
+            put(t)
+            fetch(t - 1)
+        fetch(last - 1)
+        look(0)
+        a_sb.append(to_sbuf("a_sb3", a_ps[last][:], "rows0"))
+        look(1)
+        b_sb.append(to_sbuf("b_sb3", b_ps[last], "rows1"))
+        look(2)
+        put(last)
+        for t in range(last):
+            join(t)
+        look(last)
+        halves = [(0, O // 2), (O // 2, O)]
+        for lo, hi in halves:
+            fetch(last, lo, hi)
+        for lo, hi in halves:
+            join(last, lo, hi)
+
+        hid_w = tile("hid_w", [P, O], U32)
+        hid_s = tile("hid_s", [P, O], U8)
+        for lo, hi in halves:
+            nc.vector.quantize_mx(out=hid_w[:, lo:hi].bitcast(E4M3), scales=hid_s[:, lo:hi],
+                                  in_=hid[:, lo:hi, :].rearrange("p o t -> p (o t)"))
+        for h in range(N // P):
+            cols = slice(h * P, (h + 1) * P)
+            acc = ps.tile([P, O], F32, name="o_ps%d" % h)
+            nc.tensor.matmul_mx(out=acc[:], lhsT=wb_w[:, cols].bitcast(E4M3), lhsT_scale=wb_s[:, cols],
+                                rhs=hid_w[:].bitcast(E4M3), rhs_scale=hid_s[:], start=True, stop=True)
+            res = tile("res%d" % h, [P, O], F32)
+            if h == 0:
+                nc.vector.tensor_copy(res[:], acc[:])
+                nc.sync.dma_start(out[cols, :], res[:])
+            else:
+                nc.scalar.copy(res[:], acc[:])
+                nc.scalar.dma_start(out[cols, :], res[:])

@@ -61,6 +61,8 @@ def tile_list_gatedbyslots_kernel(tc, xt_words, xt_scales, w_words, w_scales, w2
 
         xt_s = cleared_plane("xt_s", T)
         w_plane = cleared_plane("w_plane", R)
+        warm = tile("warm", [P, 1], F32)
+        nc.vector.memset(warm[:], 0.0)
 
         list1 = load_list("list1", offs)
         xt_w = tile("xt_w", [P, T], U16)
@@ -73,6 +75,8 @@ def tile_list_gatedbyslots_kernel(tc, xt_words, xt_scales, w_words, w_scales, w2
         load_plane(xt_s, xt_scales, nc.scalar)
         w_raw = load_words("w_raw", w_words, nc.sync)
         list3 = load_list("list3", offs3)
+        warm_out = tile("warm_out", [P, 1], F32)
+        nc.scalar.activation(out=warm_out[:], in_=warm[:], func=ACT.Sigmoid)
 
         def cleared_board(t, tag=""):
             page = tile("board%d" % t, [P, C], F32, tag)

@@ -45,8 +45,8 @@ def tile_list_gatedbyslots_kernel(tc, xt_words, xt_scales, w_words, w_scales, w2
             queue.dma_start(words[:].bitcast(I32), src[0].rearrange("p n t -> p (n t)").bitcast(I32))
             return words
 
-        def cleared_plane(name, cols):
-            plane = tile(name, [P, cols], U8)
+        def cleared_plane(name, cols, tag=""):
+            plane = tile(name, [P, cols], U8, tag)
             nc.vector.memset(plane[:].bitcast(I32), 0)
             return plane
 
@@ -56,11 +56,11 @@ def tile_list_gatedbyslots_kernel(tc, xt_words, xt_scales, w_words, w_scales, w2
 
         def load_per_row(name, src):
             col = tile(name, [P, PACK], F32)
-            nc.gpsimd.dma_start(col[:], src.rearrange("(p t) one -> p (t one)", t=PACK))
+            nc.sync.dma_start(col[:], src.rearrange("(p t) one -> p (t one)", t=PACK))
             return col
 
         xt_s = cleared_plane("xt_s", T)
-        w_plane = cleared_plane("w_plane", R)
+        w_plane = cleared_plane("w_plane", R, "w_plane")
         warm = tile("warm", [P, 1], F32)
         nc.vector.memset(warm[:], 0.0)
 
@@ -101,7 +101,7 @@ def tile_list_gatedbyslots_kernel(tc, xt_words, xt_scales, w_words, w_scales, w2
 
         w_first = tile("w_first", [P, P], U32, "first_words")
         nc.scalar.copy(w_first[:], w_raw[:, 0:R:PACK])
-        w_rest = tile("w_rest", [P, PACK - 1, P], U32, "rest_words")
+        w_rest = tile("w_rest", [P, PACK - 1, P], U32)
         nc.scalar.copy(w_rest[:].rearrange("p t m -> p m t"), w_raw[:].rearrange("p (m t) -> p m t", t=PACK)[:, :, 1:PACK])
         w_dealt = [w_first[:]] + [w_rest[:, t, :] for t in range(PACK - 1)]
         for q in range(QUADS):
@@ -132,7 +132,7 @@ def tile_list_gatedbyslots_kernel(tc, xt_words, xt_scales, w_words, w_scales, w2
         nc.vector.tensor_copy(w_s_late[:], w_by_slot[:, 2:4, :])
         a_ps.extend([first_product(t, w_s_late[:, t - 2, :]) for t in range(2, PACK)])
         a_sb.append(to_sbuf("a_sb2", a_ps[2][:]))
-        board.append(cleared_board(2, "rest_words"))
+        board.append(cleared_board(2, "w_plane"))
 
         xb_s = tile("xb_s", [P, J], U8, "early_scales")
         nc.vector.tensor_copy(xb_s[:], xt_s[:].indirect(list2[:]))
@@ -140,7 +140,7 @@ def tile_list_gatedbyslots_kernel(tc, xt_words, xt_scales, w_words, w_scales, w2
         nc.vector.tensor_copy(xb_w[:], xt_w[:].indirect(list2[:]))
         w2_s = tile("w2_s", [P, PACK, P], U8)
         nc.vector.tensor_copy(w2_s[:], w2_plane[:].rearrange("p (m t) -> p t m", t=PACK))
-        w2_dealt = tile("w2_dealt", [P, PACK, P], U32)
+        w2_dealt = tile("w2_dealt", [P, PACK, P], U32, "w2_dealt")
         nc.vector.tensor_copy(w2_dealt[:].bitcast(I32).rearrange("p t m -> p m t"),
                               w2_raw[:].bitcast(I32).rearrange("p (m t) -> p m t", t=PACK))
         board.append(cleared_board(3, "w2_raw"))
@@ -152,7 +152,9 @@ def tile_list_gatedbyslots_kernel(tc, xt_words, xt_scales, w_words, w_scales, w2
                 nc.tensor.matmul_mx(out=acc[:, u, :], lhsT=w2_dealt[:, t, :].bitcast(E4M3), lhsT_scale=w2_s[:, t, :],
                                     rhs=xb_w[:].bitcast(E2M1), rhs_scale=xb_s[:], start=True, stop=True)
                 b_ps.append(acc[:, u, :])
-        b_sb = [to_sbuf("b_sb%d" % t, b_ps[t], "rows%d" % t) for t in range(PACK - 1)]
+        b_sb = [to_sbuf("b_sb%d" % t, b_ps[t]) for t in range(2)]
+        a_sb.append(to_sbuf("a_sb3", a_ps[3][:], "w2_dealt"))
+        b_sb.extend([to_sbuf("b_sb%d" % t, b_ps[t]) for t in range(2, PACK)])
 
         picked = [tile("picked%d" % t, [P, O], F32) for t in range(PACK)]
         gate = [tile("gate%d" % t, [P, O], F32) for t in range(PACK)]
@@ -161,12 +163,11 @@ def tile_list_gatedbyslots_kernel(tc, xt_words, xt_scales, w_words, w_scales, w2
         def put(t):
             nc.scalar.activation(out=board[t][:].indirect(list3[:]), in_=a_sb[t][:], func=ACT.Copy)
 
-        def fetch(t, lo=0, hi=O):
-            nc.scalar.activation(out=picked[t][:, lo:hi], in_=board[t][:].indirect(list4[:, lo // 16 : hi // 16]), func=ACT.Copy,
-                                 scale=sa_t[:, t : t + 1])
+        def fetch(t):
+            nc.scalar.activation(out=picked[t][:], in_=board[t][:].indirect(list4[:]), func=ACT.Copy, scale=sa_t[:, t : t + 1])
 
-        def look(t):
-            nc.scalar.activation(out=gate[t][:], in_=b_sb[t][:].indirect(list5[:]), func=ACT.Sigmoid,
+        def look(t, lo=0, hi=O):
+            nc.scalar.activation(out=gate[t][:, lo:hi], in_=b_sb[t][:].indirect(list5[:, lo // 16 : hi // 16]), func=ACT.Sigmoid,
                                  bias=bg_t[:, t : t + 1], scale=sg_t[:, t : t + 1])
 
         def join(t, lo=0, hi=O):
@@ -179,17 +180,15 @@ def tile_list_gatedbyslots_kernel(tc, xt_words, xt_scales, w_words, w_scales, w2
             fetch(t - 1)
         fetch(last - 1)
         look(0)
-        a_sb.append(to_sbuf("a_sb3", a_ps[last][:], "rows0"))
         look(1)
-        b_sb.append(to_sbuf("b_sb3", b_ps[last], "rows1"))
-        look(2)
         put(last)
+        look(2)
+        fetch(last)
         for t in range(last):
             join(t)
-        look(last)
         halves = [(0, O // 2), (O // 2, O)]
         for lo, hi in halves:
-            fetch(last, lo, hi)
+            look(last, lo, hi)
         for lo, hi in halves:
             join(last, lo, hi)
 

@@ -63,15 +63,17 @@ def tile_list_gatedbyslots_kernel(tc, xt_words, xt_scales, w_words, w_scales, w2
         w_plane = cleared_plane("w_plane", R, "w_plane")
         warm = tile("warm", [P, 1], F32)
         nc.vector.memset(warm[:], 0.0)
+        w2_plane = cleared_plane("w2_plane", R)
+        wb_s = cleared_plane("wb_s", N)
 
         list1 = load_list("list1", offs)
-        xt_w = tile("xt_w", [P, T], U16)
-        nc.sync.dma_start(xt_w[:].bitcast(I32), xt_words[0].bitcast(I32))
         w_staged = shared.tile([P, QUADS, R // 4], I32, name="w_staged", offset=0, align_bytes=64)
-        nc.scalar.dma_start(
+        nc.sync.dma_start(
             w_staged[0:4, :, :],
             w_scales[0].bitcast(I32).rearrange("(q r) c -> r q c", r=4),
         )
+        xt_w = tile("xt_w", [P, T], U16)
+        nc.sync.dma_start(xt_w[:].bitcast(I32), xt_words[0].bitcast(I32))
         load_plane(xt_s, xt_scales, nc.scalar)
         w_raw = load_words("w_raw", w_words, nc.sync)
         list3 = load_list("list3", offs3)
@@ -83,25 +85,22 @@ def tile_list_gatedbyslots_kernel(tc, xt_words, xt_scales, w_words, w_scales, w2
             nc.vector.memset(page[:], 0.0)
             return page
 
-        board = [cleared_board(0)]
-        w2_plane = cleared_plane("w2_plane", R)
-        wb_s = cleared_plane("wb_s", N)
-        board.append(cleared_board(1))
+        board = [cleared_board(t) for t in range(2)]
 
+        load_plane(w2_plane, w2_scales, nc.sync)
+        list2 = load_list("list2", offs2)
+        w2_raw = load_words("w2_raw", w2_words, nc.sync)
         list4 = load_list("list4", offs4)
         sa_t = load_per_row("sa_t", sa)
-        load_plane(w2_plane, w2_scales, nc.sync)
-        w2_raw = load_words("w2_raw", w2_words, nc.sync, "w2_raw")
-        list2 = load_list("list2", offs2)
         list5 = load_list("list5", offs5)
         sg_t = load_per_row("sg_t", sg)
         bg_t = load_per_row("bg_t", bg)
-        wb_w = load_words("wb_w", wb_words, nc.sync)
         load_plane(wb_s, wb_scales, nc.sync)
+        wb_w = load_words("wb_w", wb_words, nc.sync)
 
         w_first = tile("w_first", [P, P], U32, "first_words")
         nc.scalar.copy(w_first[:], w_raw[:, 0:R:PACK])
-        w_rest = tile("w_rest", [P, PACK - 1, P], U32)
+        w_rest = tile("w_rest", [P, PACK - 1, P], U32, "rest_words")
         nc.scalar.copy(w_rest[:].rearrange("p t m -> p m t"), w_raw[:].rearrange("p (m t) -> p m t", t=PACK)[:, :, 1:PACK])
         w_dealt = [w_first[:]] + [w_rest[:, t, :] for t in range(PACK - 1)]
         for q in range(QUADS):
@@ -131,19 +130,19 @@ def tile_list_gatedbyslots_kernel(tc, xt_words, xt_scales, w_words, w_scales, w2
         w_s_late = tile("w_s_late", [P, 2, P], U8, "first_words")
         nc.vector.tensor_copy(w_s_late[:], w_by_slot[:, 2:4, :])
         a_ps.extend([first_product(t, w_s_late[:, t - 2, :]) for t in range(2, PACK)])
-        a_sb.append(to_sbuf("a_sb2", a_ps[2][:]))
         board.append(cleared_board(2, "w_plane"))
+        a_sb.extend([to_sbuf("a_sb%d" % t, a_ps[t][:]) for t in range(2, PACK)])
+        board.append(cleared_board(3, "rest_words"))
 
         xb_s = tile("xb_s", [P, J], U8, "early_scales")
         nc.vector.tensor_copy(xb_s[:], xt_s[:].indirect(list2[:]))
         xb_w = tile("xb_w", [P, J], U16, "first_words")
         nc.vector.tensor_copy(xb_w[:], xt_w[:].indirect(list2[:]))
-        w2_s = tile("w2_s", [P, PACK, P], U8)
+        w2_s = shared.tile([P, PACK, P], U8, name="w2_s", offset=0, align_bytes=64)
         nc.vector.tensor_copy(w2_s[:], w2_plane[:].rearrange("p (m t) -> p t m", t=PACK))
-        w2_dealt = tile("w2_dealt", [P, PACK, P], U32, "w2_dealt")
+        w2_dealt = shared.tile([P, PACK, P], U32, name="w2_dealt", offset=2 * J, align_bytes=64)
         nc.vector.tensor_copy(w2_dealt[:].bitcast(I32).rearrange("p t m -> p m t"),
                               w2_raw[:].bitcast(I32).rearrange("p (m t) -> p m t", t=PACK))
-        board.append(cleared_board(3, "w2_raw"))
         b_ps = []
         for pair in range(PACK // 2):
             acc = ps.tile([P, 2, J], F32, name="b_ps%d" % pair)
@@ -152,45 +151,42 @@ def tile_list_gatedbyslots_kernel(tc, xt_words, xt_scales, w_words, w_scales, w2
                 nc.tensor.matmul_mx(out=acc[:, u, :], lhsT=w2_dealt[:, t, :].bitcast(E4M3), lhsT_scale=w2_s[:, t, :],
                                     rhs=xb_w[:].bitcast(E2M1), rhs_scale=xb_s[:], start=True, stop=True)
                 b_ps.append(acc[:, u, :])
-        b_sb = [to_sbuf("b_sb%d" % t, b_ps[t]) for t in range(2)]
-        a_sb.append(to_sbuf("a_sb3", a_ps[3][:], "w2_dealt"))
-        b_sb.extend([to_sbuf("b_sb%d" % t, b_ps[t]) for t in range(2, PACK)])
+        b_sb = [to_sbuf("b_sb%d" % t, b_ps[t]) for t in range(PACK)]
 
-        picked = [tile("picked%d" % t, [P, O], F32) for t in range(PACK)]
-        gate = [tile("gate%d" % t, [P, O], F32) for t in range(PACK)]
+        picked = [tile("picked%d" % pair, [P, 2, O], F32) for pair in range(PACK // 2)]
+        gate = [tile("gate%d" % pair, [P, 2, O], F32) for pair in range(PACK // 2)]
         hid = tile("hid", [P, O, PACK], BF16)
 
         def put(t):
             nc.scalar.activation(out=board[t][:].indirect(list3[:]), in_=a_sb[t][:], func=ACT.Copy)
 
         def fetch(t):
-            nc.scalar.activation(out=picked[t][:], in_=board[t][:].indirect(list4[:]), func=ACT.Copy, scale=sa_t[:, t : t + 1])
+            nc.scalar.activation(out=picked[t // 2][:, t % 2, :], in_=board[t][:].indirect(list4[:]), func=ACT.Copy,
+                                 scale=sa_t[:, t : t + 1])
 
         def look(t, lo=0, hi=O):
-            nc.scalar.activation(out=gate[t][:, lo:hi], in_=b_sb[t][:].indirect(list5[:, lo // 16 : hi // 16]), func=ACT.Sigmoid,
-                                 bias=bg_t[:, t : t + 1], scale=sg_t[:, t : t + 1])
+            nc.scalar.activation(out=gate[t // 2][:, t % 2, lo:hi], in_=b_sb[t][:].indirect(list5[:, lo // 16 : hi // 16]),
+                                 func=ACT.Sigmoid, bias=bg_t[:, t : t + 1], scale=sg_t[:, t : t + 1])
 
-        def join(t, lo=0, hi=O):
-            nc.vector.tensor_tensor(hid[:, lo:hi, t], picked[t][:, lo:hi], gate[t][:, lo:hi], MULT)
+        def join(pair, lo=0, hi=O):
+            nc.vector.tensor_tensor(hid[:, lo:hi, 2 * pair : 2 * pair + 2],
+                                    picked[pair][:, :, lo:hi].rearrange("p t o -> p o t"),
+                                    gate[pair][:, :, lo:hi].rearrange("p t o -> p o t"), MULT)
 
         last = PACK - 1
         put(0)
-        for t in range(1, last):
+        for t in range(1, PACK):
             put(t)
             fetch(t - 1)
-        fetch(last - 1)
-        look(0)
-        look(1)
-        put(last)
-        look(2)
         fetch(last)
         for t in range(last):
-            join(t)
+            look(t)
+        join(0)
         halves = [(0, O // 2), (O // 2, O)]
         for lo, hi in halves:
             look(last, lo, hi)
         for lo, hi in halves:
-            join(last, lo, hi)
+            join(1, lo, hi)
 
         hid_w = tile("hid_w", [P, O], U32)
         hid_s = tile("hid_s", [P, O], U8)

@@ -60,13 +60,12 @@ def tile_list_gatedbyslots_kernel(tc, xt_words, xt_scales, w_words, w_scales, w2
             return col
 
         xt_s = cleared_plane("xt_s", T)
-        w_plane = cleared_plane("w_plane", R, "w_plane")
+        w_plane = cleared_plane("w_plane", 2 * R, "w_plane")
         warm = tile("warm", [P, 1], F32)
         nc.vector.memset(warm[:], 0.0)
         w2_plane = cleared_plane("w2_plane", R)
         wb_s = cleared_plane("wb_s", N)
 
-        list1 = load_list("list1", offs)
         w_staged = shared.tile([P, QUADS, R // 4], I32, name="w_staged", offset=0, align_bytes=64)
         nc.sync.dma_start(
             w_staged[0:4, :, :],
@@ -74,6 +73,7 @@ def tile_list_gatedbyslots_kernel(tc, xt_words, xt_scales, w_words, w_scales, w2
         )
         xt_w = tile("xt_w", [P, T], U16)
         nc.sync.dma_start(xt_w[:].bitcast(I32), xt_words[0].bitcast(I32))
+        list1 = load_list("list1", offs)
         load_plane(xt_s, xt_scales, nc.scalar)
         w_raw = load_words("w_raw", w_words, nc.sync)
         list3 = load_list("list3", offs3)
@@ -100,12 +100,16 @@ def tile_list_gatedbyslots_kernel(tc, xt_words, xt_scales, w_words, w_scales, w2
 
         w_first = tile("w_first", [P, P], U32, "first_words")
         nc.scalar.copy(w_first[:], w_raw[:, 0:R:PACK])
-        w_rest = tile("w_rest", [P, PACK - 1, P], U32, "rest_words")
-        nc.scalar.copy(w_rest[:].rearrange("p t m -> p m t"), w_raw[:].rearrange("p (m t) -> p m t", t=PACK)[:, :, 1:PACK])
-        w_dealt = [w_first[:]] + [w_rest[:, t, :] for t in range(PACK - 1)]
-        for q in range(QUADS):
-            nc.vector.tensor_copy(w_plane[QUAD * q : QUAD * q + 4, :].bitcast(I32), w_staged[0:4, q, :])
-        w_by_slot = w_plane[:].rearrange("p (m t) -> p t m", t=PACK)
+        w_second = tile("w_second", [P, P], U32)
+        nc.scalar.copy(w_second[:], w_raw[:, 1:R:PACK])
+        w_rest = tile("w_rest", [P, 2, P], U32, "rest_words")
+        nc.scalar.copy(w_rest[:].rearrange("p t m -> p m t"), w_raw[:].rearrange("p (m t) -> p m t", t=PACK)[:, :, 2:PACK])
+        w_dealt = [w_first[:], w_second[:]] + [w_rest[:, t, :] for t in range(2)]
+        spread = w_plane[:].bitcast(I32).rearrange("p (h c) -> p h c", h=2)
+        for q in range(2):
+            nc.vector.tensor_copy(spread[QUAD * q : QUAD * q + 4, :, :], w_staged[0:4, q:QUADS:2, :])
+        nc.vector.tensor_copy(spread[2 * QUAD : P, 0, :], spread[0 : 2 * QUAD, 1, :])
+        w_by_slot = w_plane[:, 0:R].rearrange("p (m t) -> p t m", t=PACK)
         w_s_early = tile("w_s_early", [P, 2, P], U8, "early_scales")
         nc.vector.tensor_copy(w_s_early[:], w_by_slot[:, 0:2, :])
 
@@ -114,24 +118,29 @@ def tile_list_gatedbyslots_kernel(tc, xt_words, xt_scales, w_words, w_scales, w2
         xa_s = shared.tile([P, J], U8, name="xa_s", offset=2 * J, align_bytes=64)
         nc.vector.tensor_copy(xa_s[:], xt_s[:].indirect(list1[:]))
 
-        def first_product(t, scales):
-            acc = ps.tile([P, J], F32, name="a_ps%d" % t)
-            nc.tensor.matmul_mx(out=acc[:], lhsT=w_dealt[t].bitcast(E5M2), lhsT_scale=scales,
-                                rhs=xa_w[:].bitcast(E2M1), rhs_scale=xa_s[:], start=True, stop=True)
-            return acc
+        def first_product(acc, t, scales, lo, hi):
+            nc.tensor.matmul_mx(out=acc, lhsT=w_dealt[t].bitcast(E5M2), lhsT_scale=scales,
+                                rhs=xa_w[:, lo:hi].bitcast(E2M1), rhs_scale=xa_s[:, lo:hi], start=True, stop=True)
 
         def to_sbuf(name, acc, tag=""):
             rows = tile(name, [P, J], F32, tag)
             nc.vector.tensor_copy(rows[:], acc)
             return rows
 
-        a_ps = [first_product(t, w_s_early[:, t, :]) for t in range(2)]
-        a_sb = [to_sbuf("a_sb%d" % t, a_ps[t][:]) for t in range(2)]
+        slot_halves = [(0, J // 2), (J // 2, J)]
+        a_sb = [tile("a_sb%d" % t, [P, J], F32) for t in range(2)]
+        for h, (lo, hi) in enumerate(slot_halves):
+            for t in range(2):
+                acc = ps.tile([P, J // 2], F32, name="a_ps%d_%d" % (t, h), tag="bank%d" % (2 * h + t))
+                first_product(acc[:], t, w_s_early[:, t, :], lo, hi)
+                nc.vector.tensor_copy(a_sb[t][:, lo:hi], acc[:])
         w_s_late = tile("w_s_late", [P, 2, P], U8, "first_words")
         nc.vector.tensor_copy(w_s_late[:], w_by_slot[:, 2:4, :])
-        a_ps.extend([first_product(t, w_s_late[:, t - 2, :]) for t in range(2, PACK)])
+        a_late = ps.tile([P, 2, J], F32, name="a_late")
+        for u in range(2):
+            first_product(a_late[:, u, :], 2 + u, w_s_late[:, u, :], 0, J)
         board.append(cleared_board(2, "w_plane"))
-        a_sb.extend([to_sbuf("a_sb%d" % t, a_ps[t][:]) for t in range(2, PACK)])
+        a_sb.extend([to_sbuf("a_sb%d" % (2 + u), a_late[:, u, :]) for u in range(2)])
         board.append(cleared_board(3, "rest_words"))
 
         xb_s = tile("xb_s", [P, J], U8, "early_scales")
@@ -157,8 +166,8 @@ def tile_list_gatedbyslots_kernel(tc, xt_words, xt_scales, w_words, w_scales, w2
         gate = [tile("gate%d" % pair, [P, 2, O], F32) for pair in range(PACK // 2)]
         hid = tile("hid", [P, O, PACK], BF16)
 
-        def put(t):
-            nc.scalar.activation(out=board[t][:].indirect(list3[:]), in_=a_sb[t][:], func=ACT.Copy)
+        def put(t, lo=0, hi=J):
+            nc.scalar.activation(out=board[t][:].indirect(list3[:, lo // 16 : hi // 16]), in_=a_sb[t][:, lo:hi], func=ACT.Copy)
 
         def fetch(t):
             nc.scalar.activation(out=picked[t // 2][:, t % 2, :], in_=board[t][:].indirect(list4[:]), func=ACT.Copy,
@@ -174,8 +183,11 @@ def tile_list_gatedbyslots_kernel(tc, xt_words, xt_scales, w_words, w_scales, w2
                                     gate[pair][:, :, lo:hi].rearrange("p t o -> p o t"), MULT)
 
         last = PACK - 1
-        put(0)
-        for t in range(1, PACK):
+        for lo, hi in slot_halves:
+            for t in range(2):
+                put(t, lo, hi)
+        fetch(0)
+        for t in range(2, PACK):
             put(t)
             fetch(t - 1)
         fetch(last)
@@ -195,7 +207,7 @@ def tile_list_gatedbyslots_kernel(tc, xt_words, xt_scales, w_words, w_scales, w2
                                   in_=hid[:, lo:hi, :].rearrange("p o t -> p (o t)"))
         for h in range(N // P):
             cols = slice(h * P, (h + 1) * P)
-            acc = ps.tile([P, O], F32, name="o_ps%d" % h)
+            acc = ps.tile([P, O], F32, name="o_ps%d" % h, tag="bank%d" % h)
             nc.tensor.matmul_mx(out=acc[:], lhsT=wb_w[:, cols].bitcast(E4M3), lhsT_scale=wb_s[:, cols],
                                 rhs=hid_w[:].bitcast(E4M3), rhs_scale=hid_s[:], start=True, stop=True)
             res = tile("res%d" % h, [P, O], F32)

from contextlib import ExitStack

import concourse.mybir as mybir

K, T, J, R, C, O, N = 512, 2048, 256, 512, 512, 128, 256
FLOPS = 2 * K * R * J * 2 + 2 * R * N * O

F32 = mybir.dt.float32
BF16 = mybir.dt.bfloat16
I32 = mybir.dt.int32
U32 = mybir.dt.uint32
U16 = mybir.dt.uint16
U8 = mybir.dt.uint8
E4M3 = mybir.dt.float8_e4m3fn_x4
E5M2 = mybir.dt.float8_e5m2_x4
E2M1 = mybir.dt.float4_e2m1fn_x4
ACT = mybir.ActivationFunctionType
MULT = mybir.AluOpType.mult

P = 128
PACK = 4
QUADS = 4
QUAD = 32


def tile_list_gatedbyslots_kernel(tc, xt_words, xt_scales, w_words, w_scales, w2_words, w2_scales, sa, sg, bg,
                                      wb_words, wb_scales, offs, offs2, offs3, offs4, offs5, out):
    nc = tc.nc
    with ExitStack() as ctx:
        sb = ctx.enter_context(tc.tile_pool(name="sb", bufs=1))
        shared = ctx.enter_context(tc.tile_pool(name="shared", bufs=1))
        ps = ctx.enter_context(tc.psum_pool(name="ps", bufs=1))

        def tile(name, shape, dtype, tag=""):
            return sb.tile(shape, dtype, name=name, tag=tag, align_bytes=64)

        def load_list(name, src):
            lst = tile(name, list(src.shape), U16)
            nc.sync.dma_start(lst[:], src)
            return lst

        def load_words(name, src, queue, tag=""):
            cols = src.shape[2]
            words = tile(name, [P, cols], U32, tag)
            queue.dma_start(words[:].bitcast(I32), src[0].rearrange("p n t -> p (n t)").bitcast(I32))
            return words

        def cleared_plane(name, cols, tag=""):
            plane = tile(name, [P, cols], U8, tag)
            nc.vector.memset(plane[:].bitcast(I32), 0)
            return plane

        def load_plane(plane, src, queue):
            for q in range(QUADS):
                queue.dma_start(plane[QUAD * q : QUAD * q + 4, :].bitcast(I32), src[0, 4 * q : 4 * q + 4, :].bitcast(I32))

        def load_per_row(name, src):
            col = tile(name, [P, PACK], F32)
            nc.sync.dma_start(col[:], src.rearrange("(p t) one -> p (t one)", t=PACK))
            return col

        xt_s = cleared_plane("xt_s", T)
        w_plane = cleared_plane("w_plane", 2 * R, "w_plane")
        warm = tile("warm", [P, 1], F32)
        nc.vector.memset(warm[:], 0.0)
        w2_plane = cleared_plane("w2_plane", R)
        wb_s = cleared_plane("wb_s", N)

        w_staged = shared.tile([P, QUADS, R // 4], I32, name="w_staged", offset=0, align_bytes=64)
        nc.sync.dma_start(
            w_staged[0:4, :, :],
            w_scales[0].bitcast(I32).rearrange("(q r) c -> r q c", r=4),
        )
        xt_w = tile("xt_w", [P, T], U16)
        nc.sync.dma_start(xt_w[:].bitcast(I32), xt_words[0].bitcast(I32))
        list1 = load_list("list1", offs)
        load_plane(xt_s, xt_scales, nc.scalar)
        w_raw = load_words("w_raw", w_words, nc.sync)
        list3 = load_list("list3", offs3)
        warm_out = tile("warm_out", [P, 1], F32)
        nc.scalar.activation(out=warm_out[:], in_=warm[:], func=ACT.Sigmoid)

        def cleared_board(t, tag=""):
            page = tile("board%d" % t, [P, C], F32, tag)
            nc.vector.memset(page[:], 0.0)
            return page

        board = [cleared_board(t) for t in range(2)]

        load_plane(w2_plane, w2_scales, nc.sync)
        list2 = load_list("list2", offs2)
        w2_raw = load_words("w2_raw", w2_words, nc.sync)
        list4 = load_list("list4", offs4)
        sa_t = load_per_row("sa_t", sa)
        list5 = load_list("list5", offs5)
        sg_t = load_per_row("sg_t", sg)
        bg_t = load_per_row("bg_t", bg)
        load_plane(wb_s, wb_scales, nc.sync)
        wb_w = load_words("wb_w", wb_words, nc.sync)

        w_first = tile("w_first", [P, P], U32, "first_words")
        nc.scalar.copy(w_first[:], w_raw[:, 0:R:PACK])
        w_second = tile("w_second", [P, P], U32)
        nc.scalar.copy(w_second[:], w_raw[:, 1:R:PACK])
        w_rest = tile("w_rest", [P, 2, P], U32, "rest_words")
        nc.scalar.copy(w_rest[:].rearrange("p t m -> p m t"), w_raw[:].rearrange("p (m t) -> p m t", t=PACK)[:, :, 2:PACK])
        w_dealt = [w_first[:], w_second[:]] + [w_rest[:, t, :] for t in range(2)]
        spread = w_plane[:].bitcast(I32).rearrange("p (h c) -> p h c", h=2)
        for q in range(2):
            nc.vector.tensor_copy(spread[QUAD * q : QUAD * q + 4, :, :], w_staged[0:4, q:QUADS:2, :])
        nc.vector.tensor_copy(spread[2 * QUAD : P, 0, :], spread[0 : 2 * QUAD, 1, :])
        w_by_slot = w_plane[:, 0:R].rearrange("p (m t) -> p t m", t=PACK)
        w_s_early = tile("w_s_early", [P, 2, P], U8, "early_scales")
        nc.vector.tensor_copy(w_s_early[:], w_by_slot[:, 0:2, :])

        xa_w = shared.tile([P, J], U16, name="xa_w", offset=0, align_bytes=64)
        nc.vector.tensor_copy(xa_w[:], xt_w[:].indirect(list1[:]))
        xa_s = shared.tile([P, J], U8, name="xa_s", offset=2 * J, align_bytes=64)
        nc.vector.tensor_copy(xa_s[:], xt_s[:].indirect(list1[:]))

        def first_product(acc, t, scales, lo, hi):
            nc.tensor.matmul_mx(out=acc, lhsT=w_dealt[t].bitcast(E5M2), lhsT_scale=scales,
                                rhs=xa_w[:, lo:hi].bitcast(E2M1), rhs_scale=xa_s[:, lo:hi], start=True, stop=True)

        def to_sbuf(name, acc, tag=""):
            rows = tile(name, [P, J], F32, tag)
            nc.vector.tensor_copy(rows[:], acc)
            return rows

        slot_halves = [(0, J // 2), (J // 2, J)]
        a_sb = [tile("a_sb%d" % t, [P, J], F32) for t in range(2)]
        for h, (lo, hi) in enumerate(slot_halves):
            for t in range(2):
                acc = ps.tile([P, J // 2], F32, name="a_ps%d_%d" % (t, h), tag="bank%d" % (2 * h + t))
                first_product(acc[:], t, w_s_early[:, t, :], lo, hi)
                nc.vector.tensor_copy(a_sb[t][:, lo:hi], acc[:])
        w_s_late = tile("w_s_late", [P, 2, P], U8, "first_words")
        nc.vector.tensor_copy(w_s_late[:], w_by_slot[:, 2:4, :])
        a_late = ps.tile([P, 2, J], F32, name="a_late")
        for u in range(2):
            first_product(a_late[:, u, :], 2 + u, w_s_late[:, u, :], 0, J)
        board.append(cleared_board(2, "w_plane"))
        a_sb.extend([to_sbuf("a_sb%d" % (2 + u), a_late[:, u, :]) for u in range(2)])
        board.append(cleared_board(3, "rest_words"))

        xb_s = tile("xb_s", [P, J], U8, "early_scales")
        nc.vector.tensor_copy(xb_s[:], xt_s[:].indirect(list2[:]))
        xb_w = tile("xb_w", [P, J], U16, "first_words")
        nc.vector.tensor_copy(xb_w[:], xt_w[:].indirect(list2[:]))
        w2_s = shared.tile([P, PACK, P], U8, name="w2_s", offset=0, align_bytes=64)
        nc.vector.tensor_copy(w2_s[:], w2_plane[:].rearrange("p (m t) -> p t m", t=PACK))
        w2_dealt = shared.tile([P, PACK, P], U32, name="w2_dealt", offset=2 * J, align_bytes=64)
        nc.vector.tensor_copy(w2_dealt[:].bitcast(I32).rearrange("p t m -> p m t"),
                              w2_raw[:].bitcast(I32).rearrange("p (m t) -> p m t", t=PACK))
        b_ps = []
        for pair in range(PACK // 2):
            acc = ps.tile([P, 2, J], F32, name="b_ps%d" % pair)
            for u in range(2):
                t = 2 * pair + u
                nc.tensor.matmul_mx(out=acc[:, u, :], lhsT=w2_dealt[:, t, :].bitcast(E4M3), lhsT_scale=w2_s[:, t, :],
                                    rhs=xb_w[:].bitcast(E2M1), rhs_scale=xb_s[:], start=True, stop=True)
                b_ps.append(acc[:, u, :])
        b_sb = [to_sbuf("b_sb%d" % t, b_ps[t]) for t in range(PACK)]

        picked = [tile("picked%d" % pair, [P, 2, O], F32) for pair in range(PACK // 2)]
        gate = [tile("gate%d" % pair, [P, 2, O], F32) for pair in range(PACK // 2)]
        hid = tile("hid", [P, O, PACK], BF16)

        def put(t, lo=0, hi=J):
            nc.scalar.activation(out=board[t][:].indirect(list3[:, lo // 16 : hi // 16]), in_=a_sb[t][:, lo:hi], func=ACT.Copy)

        def fetch(t):
            nc.scalar.activation(out=picked[t // 2][:, t % 2, :], in_=board[t][:].indirect(list4[:]), func=ACT.Copy,
                                 scale=sa_t[:, t : t + 1])

        def look(t, lo=0, hi=O):
            nc.scalar.activation(out=gate[t // 2][:, t % 2, lo:hi], in_=b_sb[t][:].indirect(list5[:, lo // 16 : hi // 16]),
                                 func=ACT.Sigmoid, bias=bg_t[:, t : t + 1], scale=sg_t[:, t : t + 1])

        def join(pair, lo=0, hi=O):
            nc.vector.tensor_tensor(hid[:, lo:hi, 2 * pair : 2 * pair + 2],
                                    picked[pair][:, :, lo:hi].rearrange("p t o -> p o t"),
                                    gate[pair][:, :, lo:hi].rearrange("p t o -> p o t"), MULT)

        last = PACK - 1
        for lo, hi in slot_halves:
            for t in range(2):
                put(t, lo, hi)
        fetch(0)
        for t in range(2, PACK):
            put(t)
            fetch(t - 1)
        fetch(last)
        for t in range(last):
            look(t)
        join(0)
        halves = [(0, O // 2), (O // 2, O)]
        for lo, hi in halves:
            look(last, lo, hi)
        for lo, hi in halves:
            join(1, lo, hi)

        hid_w = tile("hid_w", [P, O], U32)
        hid_s = tile("hid_s", [P, O], U8)
        for lo, hi in halves:
            nc.vector.quantize_mx(out=hid_w[:, lo:hi].bitcast(E4M3), scales=hid_s[:, lo:hi],
                                  in_=hid[:, lo:hi, :].rearrange("p o t -> p (o t)"))
        for h in range(N // P):
            cols = slice(h * P, (h + 1) * P)
            acc = ps.tile([P, O], F32, name="o_ps%d" % h, tag="bank%d" % h)
            nc.tensor.matmul_mx(out=acc[:], lhsT=wb_w[:, cols].bitcast(E4M3), lhsT_scale=wb_s[:, cols],
                                rhs=hid_w[:].bitcast(E4M3), rhs_scale=hid_s[:], start=True, stop=True)
            res = tile("res%d" % h, [P, O], F32)
            if h == 0:
                nc.vector.tensor_copy(res[:], acc[:])
                nc.sync.dma_start(out[cols, :], res[:])
            else:
                nc.scalar.copy(res[:], acc[:])
                nc.scalar.dma_start(out[cols, :], res[:])
